import numpy as np
import ml_dtypes


def mxq(x, axis, fmt="e4m3"):
    dtype, down = {"e4m3": (ml_dtypes.float8_e4m3fn, 7), "e5m2": (ml_dtypes.float8_e5m2, 14)}[fmt]
    v = np.moveaxis(np.asarray(x, np.float32).astype(ml_dtypes.bfloat16).astype(np.float64), axis, -1)
    blocks = v.reshape(v.shape[:-1] + (-1, 32))
    amax = np.abs(blocks).max(-1, keepdims=True)
    byte = np.maximum(np.where(amax > 0, np.frexp(amax)[1] - 1 + 127, 0) - down, 1)
    scale = np.exp2(byte - 127.0)
    codes = (blocks / scale).astype(np.float32).astype(dtype).astype(np.float64)
    return np.moveaxis((codes * scale).reshape(v.shape), -1, axis)


WIDE = False


def mx_kscale(k):
    if not WIDE:
        return np.ones(k)
    levels = np.array([10, -10, 5, -5, 0])
    if k % 512:
        return np.exp2(np.random.permutation(np.resize(levels, k // 32))).repeat(32)
    a = np.empty((k // 512, 16))
    for p in range(k // 512):
        a[p, :8] = np.random.permutation(np.resize(levels, 8))
        for g in range(8):
            far = levels[np.abs(levels - a[p, g]) >= 10]
            a[p, g + 8] = far[np.random.randint(len(far))]
    return np.exp2(a.ravel()).repeat(32)


def f64(x):
    return np.asarray(x).astype(np.float64)


def striped(idx):
    return np.tile(idx.reshape(-1, 16).T, (8, 1)).astype(np.uint16)


def unstriped(offs):
    return offs[:16].T.reshape(-1).astype(np.int64)


def striped8(idx):
    return np.concatenate([x.reshape(-1, 16).T for x in idx]).astype(np.uint16)


def runs(offs, k):
    lists = np.stack([offs[16 * r : 16 * r + 16].T.reshape(-1) for r in range(8)]).astype(np.int64)
    return lists[np.arange(k) % 512 // 64]


def pack_weight(w):
    k, n = w.shape
    w = f64(np.asarray(w, np.float32).astype(ml_dtypes.bfloat16)).reshape(k // 32, 32, n)
    amax = np.abs(w).max(1)
    byte = np.clip(np.where(amax > 0, np.frexp(amax)[1] - 1 + 127 - 7, 1), 1, 254)
    scaled = (w * np.exp2(127.0 - byte)[:, None, :]).reshape(k, n).astype(np.float32)
    words = np.ascontiguousarray(scaled.reshape(k // 512, 128, 4, n).transpose(0, 1, 3, 2)).astype(ml_dtypes.float8_e4m3fn).view(np.uint8)
    return words, np.ascontiguousarray(byte.astype(np.uint8).reshape(k // 512, 16, n))


def unpack_weight(words, scales):
    g, p, n, _ = words.shape
    vals = np.ascontiguousarray(words).view(ml_dtypes.float8_e4m3fn).astype(np.float64) * np.repeat(np.exp2(scales.astype(np.float64) - 127.0), 8, axis=1)[..., None]
    return vals.transpose(0, 1, 3, 2).reshape(g * 512, n)


def sigmoid(v):
    return 1.0 / (1.0 + np.exp(-np.maximum(v, -700.0)))


K, T, S, H = 512, 2048, 512, 512


def setup_inputs():
    n = np.random.standard_normal
    s = mx_kscale(K)[:, None]
    u = mx_kscale(S)
    packed_xT = pack_weight(n((K, T)) * s)
    return {
        "x_words": packed_xT[0],
        "x_scales": packed_xT[1],
        "wa": (n((K, H)) / np.sqrt(K) / s).astype(np.float32),
        "wb": (n((K, H)) / np.sqrt(K) / s).astype(np.float32),
        "sl": np.random.uniform(1.0, 2.0, (S, 1)).astype(np.float32),
        "th": (0.5 * n((S, 1))).astype(np.float32),
        "gt": (np.random.uniform(0.5, 1.5, (S, 1)) * u[:, None]).astype(np.float32),
        "gi": (np.random.uniform(0.5, 1.5, (S, 1)) / u[:, None]).astype(np.float32),
        "tau": np.random.uniform(0.3, 0.9, (H, 1)).astype(np.float32),
        "offs": striped(np.random.permutation(T)[:S]),
        "two": striped(np.random.permutation(T)[:S]),
        "n1": striped8(np.stack([np.random.permutation(H) for _ in range(8)])),
        "n2": striped8(np.stack([np.random.permutation(H) for _ in range(8)])),
        "n3": striped8(np.stack([np.random.permutation(H) for _ in range(8)])),
        "n4": striped8(np.stack([np.random.permutation(H) for _ in range(8)])),
    }


def reference(x_words, x_scales, wa, wb, sl, th, gt, gi, tau, offs, two, n1, n2, n3, n4):
    xq = unpack_weight(x_words, x_scales)[:, unstriped(offs)]
    a = xq.T @ mxq(f64(wa), 0, "e4m3")
    x_two = unpack_weight(x_words, x_scales)[:, unstriped(two)]
    b = x_two.T @ mxq(f64(wb), 0, "e4m3")
    sg = sigmoid(f64(sl) * (b[np.arange(S)[:, None], runs(n1, S)] - f64(th)))
    z = f64(gt) * (a * sg - (0.5 * (a[np.arange(S)[:, None], runs(n2, S)])))
    z2 = f64(gi) * b
    cv = 0.0625 * ((mxq(z, 0, "e4m3").T @ mxq(z2, 0, "e4m3")))
    top = cv.max(axis=1, keepdims=True)
    ea = np.exp(f64(tau) * (cv[np.arange(H)[:, None], runs(n3, H)] - top))
    sm = cv * ea
    ds = np.zeros((H, H))
    ds[np.arange(H)[:, None], runs(n4, H)] = sm
    return 2.0 * ds - (0.5 * cv)

@@ -1,0 +1,239 @@
+from contextlib import ExitStack
+
+import concourse.mybir as mybir
+from concourse.masks import make_identity
+
+K, T, S, H = 512, 2048, 512, 512
+FLOPS = 3 * 2 * 512 * 512 * 512
+
+F32 = mybir.dt.float32
+BF16 = mybir.dt.bfloat16
+I32 = mybir.dt.int32
+U32 = mybir.dt.uint32
+U16 = mybir.dt.uint16
+U8 = mybir.dt.uint8
+FP8X4 = mybir.dt.float8_e4m3fn_x4
+ALU = mybir.AluOpType
+ACT = mybir.ActivationFunctionType
+
+P = 128
+PACK = 4
+HALF = 256
+LIST_COLS = 32
+
+
+def tile_picked_momtgxbesd_none_p_kernel(
+    tc, x_words, x_scales, wa, wb, sl, th, gt, gi, tau, offs, two, n1, n2, n3, n4, out
+):
+    nc = tc.nc
+    with ExitStack() as ctx:
+        keep = ctx.enter_context(tc.tile_pool(name="keep", bufs=1))
+        psum = ctx.enter_context(tc.psum_pool(name="psum", bufs=1))
+
+        def sb(shape, dtype, name, slot=None):
+            return keep.tile(shape, dtype, name=name, tag=slot or name, align_bytes=64)
+
+        def bank(i, name):
+            return psum.tile([P, H], F32, name=name, tag="bank%d" % i)
+
+        def load_list(src, name):
+            lst = sb([P, LIST_COLS], U16, name)
+            nc.sync.dma_start(lst[:], src)
+            return lst
+
+        def load_column(src, name):
+            col = sb([P, PACK], F32, name)
+            nc.sync.dma_start(col[:], src.rearrange("(p t) o -> p (t o)", t=PACK))
+            return col
+
+        def load_weight_half(w, h, name):
+            raw = sb([P, PACK, HALF], F32, name)
+            nc.sync.dma_start(raw[:], w.rearrange("(p j) n -> p j n", j=PACK)[:, :, h * HALF : (h + 1) * HALF])
+            return raw
+
+        def half_list(lst, h):
+            return lst[:, h * (HALF // 16) : (h + 1) * (HALF // 16)]
+
+        xs = sb([P, T], U8, "xs")
+        nc.vector.memset(xs[:].bitcast(I32), 0)
+        two_t = load_list(two, "two_t")
+        offs_t = load_list(offs, "offs_t")
+        wb_raw = [load_weight_half(wb, 0, "wb_raw0")]
+        for q in range(4):
+            nc.sync.dma_start(xs[32 * q : 32 * q + 4, :].bitcast(I32), x_scales[0, 4 * q : 4 * q + 4, :].bitcast(I32))
+        wb_raw.append(load_weight_half(wb, 1, "wb_raw1"))
+        xw = sb([P, T], U32, "xw")
+        nc.sync.dma_start(xw[:].bitcast(I32), x_words[0].rearrange("p n t -> p (n t)").bitcast(I32))
+        sl_t = load_column(sl, "sl_t")
+        th_t = load_column(th, "th_t")
+        n1_t = load_list(n1, "n1_t")
+        gi_t = load_column(gi, "gi_t")
+        wa_raw = [load_weight_half(wa, h, "wa_raw%d" % h) for h in range(2)]
+        gt_t = load_column(gt, "gt_t")
+        n2_t = load_list(n2, "n2_t")
+        tau_t = load_column(tau, "tau_t")
+        n3_t = load_list(n3, "n3_t")
+        n4_t = load_list(n4, "n4_t")
+
+        def pick(table, lst, dtype, name):
+            picked = sb([P, PACK, P], dtype, name)
+            nc.vector.tensor_copy(picked[:].rearrange("p t m -> p m t"), table[:].indirect(lst[:]))
+            return picked
+
+        two_s = pick(xs, two_t, U8, "two_s")
+        offs_s = pick(xs, offs_t, U8, "offs_s")
+
+
+        def weave(copy, planes, name):
+            width = planes.shape[2]
+            woven = sb([P, width, PACK], BF16, name)
+            copy(
+                woven[:].rearrange("p (c i) t -> p c t i", i=4),
+                planes.rearrange("p t (c i) -> p c t i", i=4),
+            )
+            return woven
+
+        def quantize(codes, scales, woven):
+            nc.vector.quantize_mx(out=codes.bitcast(FP8X4), scales=scales, in_=woven)
+
+        def product(acc, lhs_w, lhs_s, rhs_w, rhs_s):
+            nc.tensor.matmul_mx(
+                out=acc, lhsT=lhs_w.bitcast(FP8X4), lhsT_scale=lhs_s, rhs=rhs_w.bitcast(FP8X4), rhs_scale=rhs_s,
+                start=True, stop=True,
+            )
+
+        wb_w = sb([P, H], U32, "wb_w")
+        wb_s = sb([P, H], U8, "wb_s")
+        for h in range(2):
+            woven = weave(nc.scalar.copy, wb_raw[h][:], "wb_woven%d" % h)
+            cols = slice(h * HALF, (h + 1) * HALF)
+            quantize(wb_w[:, cols], wb_s[:, cols], woven[:].rearrange("p c t -> p (c t)"))
+        sig_bias = sb([P, PACK], F32, "sig_bias")
+        nc.vector.scalar_tensor_tensor(sig_bias[:], sl_t[:], -1.0, th_t[:], ALU.mult, ALU.mult)
+        two_w = pick(xw, two_t, U32, "two_w")
+        offs_w = pick(xw, offs_t, U32, "offs_w")
+        wa_woven0 = weave(nc.vector.tensor_copy, wa_raw[0][:], "wa_woven0")
+        wa_woven1 = weave(nc.vector.tensor_copy, wa_raw[1][:], "wa_woven1")
+        wa_w = sb([P, H], U32, "wa_w")
+        wa_s = sb([P, H], U8, "wa_s")
+        quantize(wa_w[:, :HALF], wa_s[:, :HALF], wa_woven0[:].rearrange("p c t -> p (c t)"))
+        gt_half = sb([P, PACK], F32, "gt_half")
+        nc.vector.tensor_scalar(gt_half[:], gt_t[:], -0.5, None, ALU.mult)
+        quantize(wa_w[:, HALF:], wa_s[:, HALF:], wa_woven1[:].rearrange("p c t -> p (c t)"))
+
+        b_acc = [bank(t, "b_acc%d" % t) for t in range(PACK)]
+        a_acc = [bank(PACK + t, "a_acc%d" % t) for t in range(PACK)]
+        for t in range(PACK):
+            product(b_acc[t][:], two_w[:, t, :], two_s[:, t, :], wb_w[:], wb_s[:])
+        for t in range(PACK):
+            product(a_acc[t][:], offs_w[:, t, :], offs_s[:, t, :], wa_w[:], wa_s[:])
+
+        b_slots = [None, None, None, "wa_woven1"]
+        b_win = [sb([P, H], F32, "b_win%d" % t, b_slots[t]) for t in range(PACK)]
+        a_win = [sb([P, H], F32, "a_win%d" % t) for t in range(PACK)]
+        for t in range(PACK):
+            nc.vector.tensor_copy(b_win[t][:], b_acc[t][:])
+        sg = sb([P, PACK, H], F32, "sg")
+        for t in range(PACK):
+            for h in range(2):
+                nc.scalar.activation(
+                    sg[:, t, h * HALF : (h + 1) * HALF], b_win[t][:].indirect(half_list(n1_t, h)), ACT.Sigmoid,
+                    bias=sig_bias[:, t : t + 1], scale=sl_t[:, t : t + 1],
+                )
+        for t in (1, 3):
+            nc.vector.tensor_scalar(a_win[t][:], a_acc[t][:], gt_half[:, t : t + 1], None, ALU.mult)
+        for t in (0, 2):
+            nc.scalar.activation(a_win[t][:], a_acc[t][:], ACT.Copy, scale=gt_half[:, t : t + 1])
+
+
+        z2_planes = sb([P, PACK, H], BF16, "z2_planes", "wa_raw1")
+        for t in range(PACK):
+            nc.vector.tensor_scalar(z2_planes[:, t, :], b_win[t][:], gi_t[:, t : t + 1], None, ALU.mult)
+        z2_woven = weave(nc.vector.tensor_copy, z2_planes[:], "z2_woven")
+        gated = sb([P, PACK, H], F32, "gated")
+        nc.vector.scalar_tensor_tensor(gated[:, 0, :], a_win[0][:], -2.0, sg[:, 0, :], ALU.mult, ALU.mult)
+        z2_w = sb([P, H], U32, "z2_w")
+        z2_s = sb([P, H], U8, "z2_s")
+        quantize(z2_w[:], z2_s[:], z2_woven[:].rearrange("p c t -> p (c t)"))
+        for t in range(1, PACK):
+            nc.vector.scalar_tensor_tensor(gated[:, t, :], a_win[t][:], -2.0, sg[:, t, :], ALU.mult, ALU.mult)
+        tau_neg = sb([P, PACK], F32, "tau_neg")
+        nc.vector.tensor_scalar(tau_neg[:], tau_t[:], -1.0, None, ALU.mult)
+
+        fetched = sb([P, PACK, H], F32, "fetched")
+        z_woven = sb([P, PACK, P, PACK], BF16, "z_woven")
+        for lo, hi in ((0, 256), (256, 384), (384, 512)):
+            cols = slice(lo, hi)
+            for t in range(PACK):
+                nc.scalar.activation(fetched[:, t, cols], a_win[t][:].indirect(n2_t[:, lo // 16 : hi // 16]), ACT.Copy)
+            ms = slice(lo // PACK, hi // PACK)
+            nc.vector.tensor_tensor(
+                z_woven[:, :, ms, :].rearrange("p u m t -> p m u t"),
+                gated[:, :, cols].rearrange("p t (m u) -> p m u t", u=PACK),
+                fetched[:, :, cols].rearrange("p t (m u) -> p m u t", u=PACK),
+                ALU.add,
+            )
+
+        z_w = sb([P, PACK, P], U32, "z_w")
+        z_s = sb([P, PACK, P], U8, "z_s")
+        cv_acc = []
+        for u in range(PACK):
+            quantize(z_w[:, u, :], z_s[:, u, :], z_woven[:, u].rearrange("p m t -> p (m t)"))
+            acc = bank(u, "cv_acc%d" % u)
+            product(acc[:], z_w[:, u, :], z_s[:, u, :], z2_w[:], z2_s[:])
+            cv_acc.append(acc)
+
+        out_rows = out.rearrange("(m u) j -> u m j", u=PACK)
+        cv, ea = [], []
+        for u in range(PACK):
+            win = sb([P, H], F32, "cv%d" % u)
+            top = sb([P, 1], F32, "top%d" % u)
+            nc.vector.tensor_scalar(win[:], cv_acc[u][:], 0.0625, None, ALU.mult, ALU.max, accum_out=top[:])
+            exp_bias = sb([P, 1], F32, "exp_bias%d" % u)
+            nc.vector.tensor_scalar(exp_bias[:], top[:], tau_neg[:, u : u + 1], None, ALU.mult)
+            e = sb([P, H], F32, "ea%d" % u)
+            for h in range(2):
+                nc.scalar.activation(
+                    e[:, h * HALF : (h + 1) * HALF], win[:].indirect(half_list(n3_t, h)), ACT.Exp,
+                    bias=exp_bias[:], scale=tau_t[:, u : u + 1],
+                )
+            cv.append(win)
+            ea.append(e)
+
+        cv_part = []
+        for u in range(PACK):
+            part = sb([P, H], F32, "cv_part%d" % u, "exp_bias%d" % u)
+            nc.scalar.activation(part[:], cv[u][:], ACT.Copy, scale=-0.5 if u == PACK - 1 else -0.25)
+            cv_part.append(part)
+        ds = [sb([P, 2 * H], F32, "ds%d" % u) for u in range(PACK)]
+
+        def scatter(u):
+            nc.vector.tensor_tensor(ds[u][:].indirect(n4_t[:]), cv[u][:], ea[u][:], ALU.mult)
+
+        ident = sb([P, P], F32, "ident")
+        make_identity(nc, ident[:])
+
+        def finish_on_tensor(u):
+            turned = bank(PACK + (2 * u) % PACK, "turned%d" % u)
+            for c in range(PACK):
+                cols = slice(c * P, (c + 1) * P)
+                nc.tensor.matmul(turned[:, cols], cv_part[u][:, cols], ident[:], start=True, stop=False, is_transpose=True)
+                nc.tensor.matmul(turned[:, cols], ds[u][:, cols], ident[:], start=False, stop=True, is_transpose=True)
+            turned_sb = sb([P, H], F32, "turned_sb%d" % u)
+            nc.scalar.copy(turned_sb[:], turned[:])
+            back = bank(PACK + (2 * u + 1) % PACK, "back%d" % u)
+            for c in range(PACK):
+                cols = slice(c * P, (c + 1) * P)
+                nc.tensor.transpose(back[:, cols], turned_sb[:, cols], ident[:])
+            res = sb([P, H], F32, "res%d" % u)
+            nc.scalar.activation(res[:], back[:], ACT.Copy, scale=2.0)
+            nc.scalar.dma_start(out_rows[u], res[:])
+
+        for u in range(PACK - 1):
+            scatter(u)
+            finish_on_tensor(u)
+        last = PACK - 1
+        scatter(last)
+        res = sb([P, H], F32, "res%d" % last)
+        nc.vector.scalar_tensor_tensor(res[:], ds[last][:, :H], 2.0, cv_part[last][:], ALU.mult, ALU.add)
+        nc.sync.dma_start(out_rows[last], res[:])

@@ -46,11 +46,6 @@ def tile_picked_momtgxbesd_none_p_kernel(
             nc.sync.dma_start(col[:], src.rearrange("(p t) o -> p (t o)", t=PACK))
             return col
 
-        def load_weight_half(w, h, name):
-            raw = sb([P, PACK, HALF], F32, name)
-            nc.sync.dma_start(raw[:], w.rearrange("(p j) n -> p j n", j=PACK)[:, :, h * HALF : (h + 1) * HALF])
-            return raw
-
         def half_list(lst, h):
             return lst[:, h * (HALF // 16) : (h + 1) * (HALF // 16)]
 
@@ -58,20 +53,23 @@ def tile_picked_momtgxbesd_none_p_kernel(
         nc.vector.memset(xs[:].bitcast(I32), 0)
         two_t = load_list(two, "two_t")
         offs_t = load_list(offs, "offs_t")
-        wb_raw = [load_weight_half(wb, 0, "wb_raw0")]
-        for q in range(4):
-            nc.sync.dma_start(xs[32 * q : 32 * q + 4, :].bitcast(I32), x_scales[0, 4 * q : 4 * q + 4, :].bitcast(I32))
-        wb_raw.append(load_weight_half(wb, 1, "wb_raw1"))
+        wb_rows = wb.rearrange("(p j) n -> p j n", j=PACK)
+        wb_raw = [sb([P, PACK, HALF], F32, "wb_raw%d" % h) for h in range(2)]
+        nc.sync.dma_start(wb_raw[0][:], wb_rows[:, :, :HALF])
+        for r in range(4):
+            nc.sync.dma_start(xs[r:P:32, :].bitcast(I32), x_scales[0, r:16:4, :].bitcast(I32))
+        nc.sync.dma_start(wb_raw[1][:], wb_rows[:, :, HALF:])
         xw = sb([P, T], U32, "xw")
         nc.sync.dma_start(xw[:].bitcast(I32), x_words[0].rearrange("p n t -> p (n t)").bitcast(I32))
         sl_t = load_column(sl, "sl_t")
         th_t = load_column(th, "th_t")
+        wa_raw = sb([P, PACK, H], F32, "wa_raw")
+        nc.sync.dma_start(wa_raw[:], wa.rearrange("(p j) n -> p j n", j=PACK))
         n1_t = load_list(n1, "n1_t")
         gi_t = load_column(gi, "gi_t")
-        wa_raw = [load_weight_half(wa, h, "wa_raw%d" % h) for h in range(2)]
         gt_t = load_column(gt, "gt_t")
-        n2_t = load_list(n2, "n2_t")
         tau_t = load_column(tau, "tau_t")
+        n2_t = load_list(n2, "n2_t")
         n3_t = load_list(n3, "n3_t")
         n4_t = load_list(n4, "n4_t")
 
@@ -93,6 +91,11 @@ def tile_picked_momtgxbesd_none_p_kernel(
             )
             return woven
 
+        def weave_on_gpsimd(planes, name):
+            woven = sb([P, planes.shape[2], PACK], BF16, name)
+            nc.gpsimd.tensor_scalar(woven[:], planes.rearrange("p t c -> p c t"), 1.0, 0.0, ALU.mult, ALU.add)
+            return woven
+
         def quantize(codes, scales, woven):
             nc.vector.quantize_mx(out=codes.bitcast(FP8X4), scales=scales, in_=woven)
 
@@ -105,34 +108,35 @@ def tile_picked_momtgxbesd_none_p_kernel(
         wb_w = sb([P, H], U32, "wb_w")
         wb_s = sb([P, H], U8, "wb_s")
         for h in range(2):
-            woven = weave(nc.scalar.copy, wb_raw[h][:], "wb_woven%d" % h)
             cols = slice(h * HALF, (h + 1) * HALF)
+            woven = weave(nc.scalar.copy, wb_raw[h][:], "wb_woven%d" % h)
             quantize(wb_w[:, cols], wb_s[:, cols], woven[:].rearrange("p c t -> p (c t)"))
         sig_bias = sb([P, PACK], F32, "sig_bias")
         nc.vector.scalar_tensor_tensor(sig_bias[:], sl_t[:], -1.0, th_t[:], ALU.mult, ALU.mult)
         two_w = pick(xw, two_t, U32, "two_w")
         offs_w = pick(xw, offs_t, U32, "offs_w")
-        wa_woven0 = weave(nc.vector.tensor_copy, wa_raw[0][:], "wa_woven0")
-        wa_woven1 = weave(nc.vector.tensor_copy, wa_raw[1][:], "wa_woven1")
-        wa_w = sb([P, H], U32, "wa_w")
-        wa_s = sb([P, H], U8, "wa_s")
-        quantize(wa_w[:, :HALF], wa_s[:, :HALF], wa_woven0[:].rearrange("p c t -> p (c t)"))
-        gt_half = sb([P, PACK], F32, "gt_half")
-        nc.vector.tensor_scalar(gt_half[:], gt_t[:], -0.5, None, ALU.mult)
-        quantize(wa_w[:, HALF:], wa_s[:, HALF:], wa_woven1[:].rearrange("p c t -> p (c t)"))
 
         b_acc = [bank(t, "b_acc%d" % t) for t in range(PACK)]
         a_acc = [bank(PACK + t, "a_acc%d" % t) for t in range(PACK)]
+        b_win = [sb([P, H], F32, "b_win%d" % t) for t in range(PACK - 1)]
+        a_win = [sb([P, H], F32, "a_win%d" % t) for t in range(PACK)]
         for t in range(PACK):
             product(b_acc[t][:], two_w[:, t, :], two_s[:, t, :], wb_w[:], wb_s[:])
+        for t in range(PACK - 1):
+            nc.vector.tensor_copy(b_win[t][:], b_acc[t][:])
+        wa_woven = [
+            weave(nc.vector.tensor_copy, wa_raw[:, :, h * HALF : (h + 1) * HALF], "wa_woven%d" % h) for h in range(2)
+        ]
+        wa_w = sb([P, H], U32, "wa_w")
+        wa_s = sb([P, H], U8, "wa_s")
+        for h in range(2):
+            cols = slice(h * HALF, (h + 1) * HALF)
+            quantize(wa_w[:, cols], wa_s[:, cols], wa_woven[h][:].rearrange("p c t -> p (c t)"))
+        b_win.append(sb([P, H], F32, "b_win3", "wa_woven1"))
+        nc.vector.tensor_copy(b_win[3][:], b_acc[3][:])
         for t in range(PACK):
             product(a_acc[t][:], offs_w[:, t, :], offs_s[:, t, :], wa_w[:], wa_s[:])
 
-        b_slots = [None, None, None, "wa_woven1"]
-        b_win = [sb([P, H], F32, "b_win%d" % t, b_slots[t]) for t in range(PACK)]
-        a_win = [sb([P, H], F32, "a_win%d" % t) for t in range(PACK)]
-        for t in range(PACK):
-            nc.vector.tensor_copy(b_win[t][:], b_acc[t][:])
         sg = sb([P, PACK, H], F32, "sg")
         for t in range(PACK):
             for h in range(2):
@@ -140,25 +144,25 @@ def tile_picked_momtgxbesd_none_p_kernel(
                     sg[:, t, h * HALF : (h + 1) * HALF], b_win[t][:].indirect(half_list(n1_t, h)), ACT.Sigmoid,
                     bias=sig_bias[:, t : t + 1], scale=sl_t[:, t : t + 1],
                 )
-        for t in (1, 3):
-            nc.vector.tensor_scalar(a_win[t][:], a_acc[t][:], gt_half[:, t : t + 1], None, ALU.mult)
-        for t in (0, 2):
-            nc.scalar.activation(a_win[t][:], a_acc[t][:], ACT.Copy, scale=gt_half[:, t : t + 1])
-
-
-        z2_planes = sb([P, PACK, H], BF16, "z2_planes", "wa_raw1")
+        gt_half = sb([P, PACK], F32, "gt_half")
+        nc.vector.tensor_scalar(gt_half[:], gt_t[:], -0.5, None, ALU.mult)
+        z2_planes = sb([P, PACK, H], BF16, "z2_planes", "wa_raw")
         for t in range(PACK):
             nc.vector.tensor_scalar(z2_planes[:, t, :], b_win[t][:], gi_t[:, t : t + 1], None, ALU.mult)
-        z2_woven = weave(nc.vector.tensor_copy, z2_planes[:], "z2_woven")
-        gated = sb([P, PACK, H], F32, "gated")
-        nc.vector.scalar_tensor_tensor(gated[:, 0, :], a_win[0][:], -2.0, sg[:, 0, :], ALU.mult, ALU.mult)
+        z2_woven = [weave_on_gpsimd(z2_planes[:, :, h * HALF : (h + 1) * HALF], "z2_woven%d" % h) for h in range(2)]
+        for t in range(PACK):
+            nc.vector.tensor_scalar(a_win[t][:], a_acc[t][:], gt_half[:, t : t + 1], None, ALU.mult)
+
+        gated = sb([P, PACK, H], F32, "gated", "gt_half")
+        for t in range(PACK):
+            nc.vector.scalar_tensor_tensor(
+                gated[:, t, :], a_acc[t][:], gt_t[:, t : t + 1], sg[:, t, :], ALU.mult, ALU.mult
+            )
         z2_w = sb([P, H], U32, "z2_w")
         z2_s = sb([P, H], U8, "z2_s")
-        quantize(z2_w[:], z2_s[:], z2_woven[:].rearrange("p c t -> p (c t)"))
-        for t in range(1, PACK):
-            nc.vector.scalar_tensor_tensor(gated[:, t, :], a_win[t][:], -2.0, sg[:, t, :], ALU.mult, ALU.mult)
-        tau_neg = sb([P, PACK], F32, "tau_neg")
-        nc.vector.tensor_scalar(tau_neg[:], tau_t[:], -1.0, None, ALU.mult)
+        for h in range(2):
+            cols = slice(h * HALF, (h + 1) * HALF)
+            quantize(z2_w[:, cols], z2_s[:, cols], z2_woven[h][:].rearrange("p c t -> p (c t)"))
 
         fetched = sb([P, PACK, H], F32, "fetched")
         z_woven = sb([P, PACK, P, PACK], BF16, "z_woven")
@@ -168,9 +172,9 @@ def tile_picked_momtgxbesd_none_p_kernel(
                 nc.scalar.activation(fetched[:, t, cols], a_win[t][:].indirect(n2_t[:, lo // 16 : hi // 16]), ACT.Copy)
             ms = slice(lo // PACK, hi // PACK)
             nc.vector.tensor_tensor(
-                z_woven[:, :, ms, :].rearrange("p u m t -> p m u t"),
-                gated[:, :, cols].rearrange("p t (m u) -> p m u t", u=PACK),
-                fetched[:, :, cols].rearrange("p t (m u) -> p m u t", u=PACK),
+                z_woven[:, :, ms, :].rearrange("p u m t -> p m t u"),
+                gated[:, :, cols].rearrange("p t (m u) -> p m t u", u=PACK),
+                fetched[:, :, cols].rearrange("p t (m u) -> p m t u", u=PACK),
                 ALU.add,
             )
 
@@ -190,7 +194,7 @@ def tile_picked_momtgxbesd_none_p_kernel(
             top = sb([P, 1], F32, "top%d" % u)
             nc.vector.tensor_scalar(win[:], cv_acc[u][:], 0.0625, None, ALU.mult, ALU.max, accum_out=top[:])
             exp_bias = sb([P, 1], F32, "exp_bias%d" % u)
-            nc.vector.tensor_scalar(exp_bias[:], top[:], tau_neg[:, u : u + 1], None, ALU.mult)
+            nc.vector.tensor_scalar(exp_bias[:], top[:], tau_t[:, u : u + 1], -1.0, ALU.mult, ALU.mult)
             e = sb([P, H], F32, "ea%d" % u)
             for h in range(2):
                 nc.scalar.activation(
@@ -235,5 +239,7 @@ def tile_picked_momtgxbesd_none_p_kernel(
         last = PACK - 1
         scatter(last)
         res = sb([P, H], F32, "res%d" % last)
-        nc.vector.scalar_tensor_tensor(res[:], ds[last][:, :H], 2.0, cv_part[last][:], ALU.mult, ALU.add)
-        nc.sync.dma_start(out_rows[last], res[:])
+        for h in range(2):
+            cols = slice(h * HALF, (h + 1) * HALF)
+            nc.vector.scalar_tensor_tensor(res[:, cols], ds[last][:, cols], 2.0, cv_part[last][:, cols], ALU.mult, ALU.add)
+            nc.sync.dma_start(out_rows[last][:, cols], res[:, cols])

@@ -61,11 +61,11 @@ def tile_picked_momtgxbesd_none_p_kernel(
         nc.sync.dma_start(wb_raw[1][:], wb_rows[:, :, HALF:])
         xw = sb([P, T], U32, "xw")
         nc.sync.dma_start(xw[:].bitcast(I32), x_words[0].rearrange("p n t -> p (n t)").bitcast(I32))
+        n1_t = load_list(n1, "n1_t")
         sl_t = load_column(sl, "sl_t")
         th_t = load_column(th, "th_t")
         wa_raw = sb([P, PACK, H], F32, "wa_raw")
         nc.sync.dma_start(wa_raw[:], wa.rearrange("(p j) n -> p j n", j=PACK))
-        n1_t = load_list(n1, "n1_t")
         gi_t = load_column(gi, "gi_t")
         gt_t = load_column(gt, "gt_t")
         tau_t = load_column(tau, "tau_t")
@@ -150,10 +150,11 @@ def tile_picked_momtgxbesd_none_p_kernel(
         for t in range(PACK):
             nc.vector.tensor_scalar(z2_planes[:, t, :], b_win[t][:], gi_t[:, t : t + 1], None, ALU.mult)
         z2_woven = [weave_on_gpsimd(z2_planes[:, :, h * HALF : (h + 1) * HALF], "z2_woven%d" % h) for h in range(2)]
-        for t in range(PACK):
-            nc.vector.tensor_scalar(a_win[t][:], a_acc[t][:], gt_half[:, t : t + 1], None, ALU.mult)
+        for t in range(0, PACK, 2):
+            nc.scalar.activation(a_win[t][:], a_acc[t][:], ACT.Copy, scale=gt_half[:, t : t + 1])
+            nc.vector.tensor_scalar(a_win[t + 1][:], a_acc[t + 1][:], gt_half[:, t + 1 : t + 2], None, ALU.mult)
 
-        gated = sb([P, PACK, H], F32, "gated", "gt_half")
+        gated = sb([P, PACK, H], F32, "gated")
         for t in range(PACK):
             nc.vector.scalar_tensor_tensor(
                 gated[:, t, :], a_acc[t][:], gt_t[:, t : t + 1], sg[:, t, :], ALU.mult, ALU.mult

from contextlib import ExitStack

import concourse.mybir as mybir
from concourse.masks import make_identity

K, T, S, H = 512, 2048, 512, 512
FLOPS = 3 * 2 * 512 * 512 * 512

F32 = mybir.dt.float32
BF16 = mybir.dt.bfloat16
I32 = mybir.dt.int32
U32 = mybir.dt.uint32
U16 = mybir.dt.uint16
U8 = mybir.dt.uint8
FP8X4 = mybir.dt.float8_e4m3fn_x4
ALU = mybir.AluOpType
ACT = mybir.ActivationFunctionType

P = 128
PACK = 4
HALF = 256
LIST_COLS = 32


def tile_picked_momtgxbesd_none_p_kernel(
    tc, x_words, x_scales, wa, wb, sl, th, gt, gi, tau, offs, two, n1, n2, n3, n4, out
):
    nc = tc.nc
    with ExitStack() as ctx:
        keep = ctx.enter_context(tc.tile_pool(name="keep", bufs=1))
        psum = ctx.enter_context(tc.psum_pool(name="psum", bufs=1))

        def sb(shape, dtype, name, slot=None):
            return keep.tile(shape, dtype, name=name, tag=slot or name, align_bytes=64)

        def bank(i, name):
            return psum.tile([P, H], F32, name=name, tag="bank%d" % i)

        def load_list(src, name):
            lst = sb([P, LIST_COLS], U16, name)
            nc.sync.dma_start(lst[:], src)
            return lst

        def load_column(src, name):
            col = sb([P, PACK], F32, name)
            nc.sync.dma_start(col[:], src.rearrange("(p t) o -> p (t o)", t=PACK))
            return col

        def half_list(lst, h):
            return lst[:, h * (HALF // 16) : (h + 1) * (HALF // 16)]

        xs = sb([P, T], U8, "xs")
        nc.vector.memset(xs[:].bitcast(I32), 0)
        two_t = load_list(two, "two_t")
        offs_t = load_list(offs, "offs_t")
        wb_rows = wb.rearrange("(p j) n -> p j n", j=PACK)
        wb_raw = [sb([P, PACK, HALF], F32, "wb_raw%d" % h) for h in range(2)]
        nc.sync.dma_start(wb_raw[0][:], wb_rows[:, :, :HALF])
        for r in range(4):
            nc.sync.dma_start(xs[r:P:32, :].bitcast(I32), x_scales[0, r:16:4, :].bitcast(I32))
        nc.sync.dma_start(wb_raw[1][:], wb_rows[:, :, HALF:])
        xw = sb([P, T], U32, "xw")
        nc.sync.dma_start(xw[:].bitcast(I32), x_words[0].rearrange("p n t -> p (n t)").bitcast(I32))
        n1_t = load_list(n1, "n1_t")
        sl_t = load_column(sl, "sl_t")
        th_t = load_column(th, "th_t")
        wa_raw = sb([P, PACK, H], F32, "wa_raw")
        nc.sync.dma_start(wa_raw[:], wa.rearrange("(p j) n -> p j n", j=PACK))
        gi_t = load_column(gi, "gi_t")
        gt_t = load_column(gt, "gt_t")
        tau_t = load_column(tau, "tau_t")
        n2_t = load_list(n2, "n2_t")
        n3_t = load_list(n3, "n3_t")
        n4_t = load_list(n4, "n4_t")

        def pick(table, lst, dtype, name):
            picked = sb([P, PACK, P], dtype, name)
            nc.vector.tensor_copy(picked[:].rearrange("p t m -> p m t"), table[:].indirect(lst[:]))
            return picked

        two_s = pick(xs, two_t, U8, "two_s")
        offs_s = pick(xs, offs_t, U8, "offs_s")


        def weave(copy, planes, name):
            width = planes.shape[2]
            woven = sb([P, width, PACK], BF16, name)
            copy(
                woven[:].rearrange("p (c i) t -> p c t i", i=4),
                planes.rearrange("p t (c i) -> p c t i", i=4),
            )
            return woven

        def weave_on_gpsimd(planes, name):
            woven = sb([P, planes.shape[2], PACK], BF16, name)
            nc.gpsimd.tensor_scalar(woven[:], planes.rearrange("p t c -> p c t"), 1.0, 0.0, ALU.mult, ALU.add)
            return woven

        def quantize(codes, scales, woven):
            nc.vector.quantize_mx(out=codes.bitcast(FP8X4), scales=scales, in_=woven)

        def product(acc, lhs_w, lhs_s, rhs_w, rhs_s):
            nc.tensor.matmul_mx(
                out=acc, lhsT=lhs_w.bitcast(FP8X4), lhsT_scale=lhs_s, rhs=rhs_w.bitcast(FP8X4), rhs_scale=rhs_s,
                start=True, stop=True,
            )

        wb_w = sb([P, H], U32, "wb_w")
        wb_s = sb([P, H], U8, "wb_s")
        for h in range(2):
            cols = slice(h * HALF, (h + 1) * HALF)
            woven = weave(nc.scalar.copy, wb_raw[h][:], "wb_woven%d" % h)
            quantize(wb_w[:, cols], wb_s[:, cols], woven[:].rearrange("p c t -> p (c t)"))
        sig_bias = sb([P, PACK], F32, "sig_bias")
        nc.vector.scalar_tensor_tensor(sig_bias[:], sl_t[:], -1.0, th_t[:], ALU.mult, ALU.mult)
        two_w = pick(xw, two_t, U32, "two_w")
        offs_w = pick(xw, offs_t, U32, "offs_w")

        b_acc = [bank(t, "b_acc%d" % t) for t in range(PACK)]
        a_acc = [bank(PACK + t, "a_acc%d" % t) for t in range(PACK)]
        b_win = [sb([P, H], F32, "b_win%d" % t) for t in range(PACK - 1)]
        a_win = [sb([P, H], F32, "a_win%d" % t) for t in range(PACK)]
        for t in range(PACK):
            product(b_acc[t][:], two_w[:, t, :], two_s[:, t, :], wb_w[:], wb_s[:])
        for t in range(PACK - 1):
            nc.vector.tensor_copy(b_win[t][:], b_acc[t][:])
        wa_woven = [
            weave(nc.vector.tensor_copy, wa_raw[:, :, h * HALF : (h + 1) * HALF], "wa_woven%d" % h) for h in range(2)
        ]
        wa_w = sb([P, H], U32, "wa_w")
        wa_s = sb([P, H], U8, "wa_s")
        for h in range(2):
            cols = slice(h * HALF, (h + 1) * HALF)
            quantize(wa_w[:, cols], wa_s[:, cols], wa_woven[h][:].rearrange("p c t -> p (c t)"))
        b_win.append(sb([P, H], F32, "b_win3", "wa_woven1"))
        nc.vector.tensor_copy(b_win[3][:], b_acc[3][:])
        for t in range(PACK):
            product(a_acc[t][:], offs_w[:, t, :], offs_s[:, t, :], wa_w[:], wa_s[:])

        sg = sb([P, PACK, H], F32, "sg")
        for t in range(PACK):
            for h in range(2):
                nc.scalar.activation(
                    sg[:, t, h * HALF : (h + 1) * HALF], b_win[t][:].indirect(half_list(n1_t, h)), ACT.Sigmoid,
                    bias=sig_bias[:, t : t + 1], scale=sl_t[:, t : t + 1],
                )
        gt_half = sb([P, PACK], F32, "gt_half")
        nc.vector.tensor_scalar(gt_half[:], gt_t[:], -0.5, None, ALU.mult)
        z2_planes = sb([P, PACK, H], BF16, "z2_planes", "wa_raw")
        for t in range(PACK):
            nc.vector.tensor_scalar(z2_planes[:, t, :], b_win[t][:], gi_t[:, t : t + 1], None, ALU.mult)
        z2_woven = [weave_on_gpsimd(z2_planes[:, :, h * HALF : (h + 1) * HALF], "z2_woven%d" % h) for h in range(2)]
        for t in range(0, PACK, 2):
            nc.scalar.activation(a_win[t][:], a_acc[t][:], ACT.Copy, scale=gt_half[:, t : t + 1])
            nc.vector.tensor_scalar(a_win[t + 1][:], a_acc[t + 1][:], gt_half[:, t + 1 : t + 2], None, ALU.mult)

        gated = sb([P, PACK, H], F32, "gated")
        for t in range(PACK):
            nc.vector.scalar_tensor_tensor(
                gated[:, t, :], a_acc[t][:], gt_t[:, t : t + 1], sg[:, t, :], ALU.mult, ALU.mult
            )
        z2_w = sb([P, H], U32, "z2_w")
        z2_s = sb([P, H], U8, "z2_s")
        for h in range(2):
            cols = slice(h * HALF, (h + 1) * HALF)
            quantize(z2_w[:, cols], z2_s[:, cols], z2_woven[h][:].rearrange("p c t -> p (c t)"))

        fetched = sb([P, PACK, H], F32, "fetched")
        z_woven = sb([P, PACK, P, PACK], BF16, "z_woven")
        for lo, hi in ((0, 256), (256, 384), (384, 512)):
            cols = slice(lo, hi)
            for t in range(PACK):
                nc.scalar.activation(fetched[:, t, cols], a_win[t][:].indirect(n2_t[:, lo // 16 : hi // 16]), ACT.Copy)
            ms = slice(lo // PACK, hi // PACK)
            nc.vector.tensor_tensor(
                z_woven[:, :, ms, :].rearrange("p u m t -> p m t u"),
                gated[:, :, cols].rearrange("p t (m u) -> p m t u", u=PACK),
                fetched[:, :, cols].rearrange("p t (m u) -> p m t u", u=PACK),
                ALU.add,
            )

        z_w = sb([P, PACK, P], U32, "z_w")
        z_s = sb([P, PACK, P], U8, "z_s")
        cv_acc = []
        for u in range(PACK):
            quantize(z_w[:, u, :], z_s[:, u, :], z_woven[:, u].rearrange("p m t -> p (m t)"))
            acc = bank(u, "cv_acc%d" % u)
            product(acc[:], z_w[:, u, :], z_s[:, u, :], z2_w[:], z2_s[:])
            cv_acc.append(acc)

        out_rows = out.rearrange("(m u) j -> u m j", u=PACK)
        cv, ea = [], []
        for u in range(PACK):
            win = sb([P, H], F32, "cv%d" % u)
            top = sb([P, 1], F32, "top%d" % u)
            nc.vector.tensor_scalar(win[:], cv_acc[u][:], 0.0625, None, ALU.mult, ALU.max, accum_out=top[:])
            exp_bias = sb([P, 1], F32, "exp_bias%d" % u)
            nc.vector.tensor_scalar(exp_bias[:], top[:], tau_t[:, u : u + 1], -1.0, ALU.mult, ALU.mult)
            e = sb([P, H], F32, "ea%d" % u)
            for h in range(2):
                nc.scalar.activation(
                    e[:, h * HALF : (h + 1) * HALF], win[:].indirect(half_list(n3_t, h)), ACT.Exp,
                    bias=exp_bias[:], scale=tau_t[:, u : u + 1],
                )
            cv.append(win)
            ea.append(e)

        cv_part = []
        for u in range(PACK):
            part = sb([P, H], F32, "cv_part%d" % u, "exp_bias%d" % u)
            nc.scalar.activation(part[:], cv[u][:], ACT.Copy, scale=-0.5 if u == PACK - 1 else -0.25)
            cv_part.append(part)
        ds = [sb([P, 2 * H], F32, "ds%d" % u) for u in range(PACK)]

        def scatter(u):
            nc.vector.tensor_tensor(ds[u][:].indirect(n4_t[:]), cv[u][:], ea[u][:], ALU.mult)

        ident = sb([P, P], F32, "ident")
        make_identity(nc, ident[:])

        def finish_on_tensor(u):
            turned = bank(PACK + (2 * u) % PACK, "turned%d" % u)
            for c in range(PACK):
                cols = slice(c * P, (c + 1) * P)
                nc.tensor.matmul(turned[:, cols], cv_part[u][:, cols], ident[:], start=True, stop=False, is_transpose=True)
                nc.tensor.matmul(turned[:, cols], ds[u][:, cols], ident[:], start=False, stop=True, is_transpose=True)
            turned_sb = sb([P, H], F32, "turned_sb%d" % u)
            nc.scalar.copy(turned_sb[:], turned[:])
            back = bank(PACK + (2 * u + 1) % PACK, "back%d" % u)
            for c in range(PACK):
                cols = slice(c * P, (c + 1) * P)
                nc.tensor.transpose(back[:, cols], turned_sb[:, cols], ident[:])
            res = sb([P, H], F32, "res%d" % u)
            nc.scalar.activation(res[:], back[:], ACT.Copy, scale=2.0)
            nc.scalar.dma_start(out_rows[u], res[:])

        for u in range(PACK - 1):
            scatter(u)
            finish_on_tensor(u)
        last = PACK - 1
        scatter(last)
        res = sb([P, H], F32, "res%d" % last)
        for h in range(2):
            cols = slice(h * HALF, (h + 1) * HALF)
            nc.vector.scalar_tensor_tensor(res[:, cols], ds[last][:, cols], 2.0, cv_part[last][:, cols], ALU.mult, ALU.add)
            nc.sync.dma_start(out_rows[last][:, cols], res[:, cols])
